import numpy as np
import ml_dtypes


def mxq(x, axis, fmt="e4m3"):
    dtype, down = {"e4m3": (ml_dtypes.float8_e4m3fn, 7), "e5m2": (ml_dtypes.float8_e5m2, 14)}[fmt]
    v = np.moveaxis(np.asarray(x, np.float32).astype(ml_dtypes.bfloat16).astype(np.float64), axis, -1)
    blocks = v.reshape(v.shape[:-1] + (-1, 32))
    amax = np.abs(blocks).max(-1, keepdims=True)
    byte = np.maximum(np.where(amax > 0, np.frexp(amax)[1] - 1 + 127, 0) - down, 1)
    scale = np.exp2(byte - 127.0)
    codes = (blocks / scale).astype(np.float32).astype(dtype).astype(np.float64)
    return np.moveaxis((codes * scale).reshape(v.shape), -1, axis)


WIDE = False


def mx_kscale(k):
    if not WIDE:
        return np.ones(k)
    levels = np.array([10, -10, 5, -5, 0])
    if k % 512:
        return np.exp2(np.random.permutation(np.resize(levels, k // 32))).repeat(32)
    a = np.empty((k // 512, 16))
    for p in range(k // 512):
        a[p, :8] = np.random.permutation(np.resize(levels, 8))
        for g in range(8):
            far = levels[np.abs(levels - a[p, g]) >= 10]
            a[p, g + 8] = far[np.random.randint(len(far))]
    return np.exp2(a.ravel()).repeat(32)


def f64(x):
    return np.asarray(x).astype(np.float64)


def striped(idx):
    return np.tile(np.asarray(idx).reshape(-1, 16).T, (8, 1)).astype(np.uint16)


def unstriped(offs):
    return offs[:16].T.reshape(-1).astype(np.int64)


B, N, C, D, NQ = 1, 2048, 4096, 512, 128


def eight(codes):
    return np.concatenate([codes[h].reshape(-1, 16).T for h in range(8)]).astype(np.uint16)


def uneight(offs):
    return np.stack([offs[16 * h:16 * h + 16].T.reshape(-1) for h in range(8)]).astype(np.int64)


def setup_inputs():
    n = np.random.standard_normal
    s = mx_kscale(D)[:, None]
    grid = lambda x: np.round(x * 32) / 32
    return {
        "qT": (n((B, D, NQ)) * s / np.sqrt(D)).astype(np.float32),
        "cb": (grid(n((D, C))) / s).astype(np.float32),
        "norm": np.tile(np.random.randint(32, 129, N) / 64.0, (128, 1)).astype(np.float32),
        "bias": np.tile(n(N), (128, 1)).astype(np.float32),
        "offs": eight(np.random.randint(0, C, (8, N))),
    }


def reference(qT, cb, norm, bias, offs):
    k = []
    for part, offs_ in enumerate((offs,)):
        codes = uneight(offs_)
        k += [f64(cb)[512 * part + 64 * h:512 * part + 64 * h + 64][:, codes[h]] for h in range(8)]
    k = np.concatenate(k) * f64(norm)[:1]
    a = mxq(f64(qT), 1, "e4m3").transpose(0, 2, 1) @ mxq(k, 0, "e4m3")
    a = a + f64(bias)[:1]
    return a

@@ -1,0 +1,145 @@
+import concourse.mybir as mybir
+from concourse.masks import make_identity
+
+F32 = mybir.dt.float32
+BF16 = mybir.dt.bfloat16
+U32 = mybir.dt.uint32
+U16 = mybir.dt.uint16
+U8 = mybir.dt.uint8
+FP8X4 = mybir.dt.float8_e4m3fn_x4
+MULT = mybir.AluOpType.mult
+ADD = mybir.AluOpType.add
+
+P = 128
+D = 512
+N = 2048
+C = 4096
+NQ = 128
+PACK = 4
+
+FLOPS = 2 * NQ * D * N
+BYTES = 4 * (D * C + D * NQ + 2 * N + NQ * N) + 2 * 8 * N
+
+CHUNKS = ((0, 512), (512, 1024), (1024, 1536), (1536, 1792), (1792, 2048))
+
+
+def tile_attend_pq_lin_bias_kernel(tc, qT, cb, norm, bias, offs, out):
+    nc = tc.nc
+    with (
+        tc.tile_pool(name="held", bufs=1) as held,
+        tc.psum_pool(name="psum", bufs=1) as psum,
+    ):
+        norm16 = held.tile([P, 2, 8], F32, name="norm16")
+        nc.sync.dma_start(out=norm16[:], in_=norm[0:1, :].rearrange("o (b p m) -> p (o b) m", b=2, m=8))
+        offsets = held.tile([P, N // 16], U16, name="offsets")
+        nc.sync.dma_start(offsets[:], offs)
+
+        planes = []
+        rows = cb.rearrange("(p t) c -> p t c", t=PACK)
+        for t in range(PACK):
+            plane = held.tile([P, C], F32, name=f"plane{t}")
+            nc.sync.dma_start(out=plane[:], in_=rows[:, t, :])
+            planes.append(plane)
+        q_raw = held.tile([P, PACK, NQ], F32, name="q_raw")
+        nc.sync.dma_start(out=q_raw[:], in_=qT[0].rearrange("(p t) q -> p t q", t=PACK))
+        bias_sb = held.tile([P, N], F32, name="bias_sb")
+        nc.sync.dma_start(out=bias_sb[:], in_=bias)
+
+        ident = held.tile([P, P], F32, name="ident")
+        make_identity(nc, ident[:])
+        norm_rep = held.tile([P, N], F32, name="norm_rep")
+        norm_view = norm_rep[:].rearrange("p (b j h m) -> p b h j m", b=2, h=2, m=4)
+        for b in range(2):
+            for h in range(2):
+                bank = psum.tile([P, 4, P], F32, name=f"norm_bank{b}{h}")
+                for m in range(4):
+                    col = norm16[:, b, 4 * h + m : 4 * h + m + 1]
+                    nc.tensor.transpose(bank[:, m, :], col.to_broadcast([P, P]), ident[:])
+                if b == 0:
+                    nc.vector.tensor_copy(out=norm_view[:, b, h], in_=bank[:].rearrange("p m j -> p j m"))
+                else:
+                    nc.scalar.copy(out=norm_view[:, b, h], in_=bank[:].rearrange("p m j -> p j m"))
+
+        pairs = [held.tile([P, 2, N], F32, name=f"pair{h}") for h in range(2)]
+        grouped, codes, scales = [], [], []
+        for i, (lo, hi) in enumerate(CHUNKS):
+            grouped.append(held.tile([P, hi - lo, PACK], BF16, name=f"grouped{i}", align_bytes=64))
+            codes.append(held.tile([P, hi - lo], U32, name=f"codes{i}", align_bytes=64))
+            scales.append(held.tile([P, hi - lo], U8, name=f"scales{i}", align_bytes=64))
+
+        def gather(t, lo, hi):
+            nc.vector.tensor_tensor(
+                pairs[t // 2][:, t % 2, lo:hi],
+                planes[t][:].indirect(offsets[:, lo // 16 : hi // 16]),
+                norm_rep[:, lo:hi],
+                MULT,
+            )
+
+        def round_pair(h, i):
+            lo, hi = CHUNKS[i]
+            nc.scalar.copy(
+                out=grouped[i][:, :, 2 * h : 2 * h + 2],
+                in_=pairs[h][:, :, lo:hi].rearrange("p t c -> p c t"),
+            )
+
+        for t in range(3):
+            for lo in range(0, N, 1024):
+                gather(t, lo, lo + 1024)
+            if t == 1:
+                for i in range(len(CHUNKS)):
+                    round_pair(0, i)
+
+        q_grouped = held.tile([P, NQ, PACK], BF16, name="q_grouped", align_bytes=64)
+        nc.scalar.copy(out=q_grouped[:], in_=q_raw[:].rearrange("p t q -> p q t"))
+        q_codes = held.tile([P, NQ], U32, name="q_codes", align_bytes=64)
+        q_scales = held.tile([P, NQ], U8, name="q_scales", align_bytes=64)
+
+        def quantize_q():
+            nc.vector.quantize_mx(
+                out=q_codes[:].bitcast(FP8X4),
+                scales=q_scales[:],
+                in_=q_grouped[:].rearrange("p q t -> p (q t)"),
+            )
+
+        result = [held.tile([P, hi - lo], F32, name=f"result{i}") for i, (lo, hi) in enumerate(CHUNKS)]
+
+        def quantize(i):
+            nc.vector.quantize_mx(
+                out=codes[i][:].bitcast(FP8X4),
+                scales=scales[i][:],
+                in_=grouped[i][:].rearrange("p c t -> p (c t)"),
+            )
+
+        accs = {}
+
+        def multiply(i):
+            lo, hi = CHUNKS[i]
+            acc = psum.tile([P, 512], F32, name="acc", tag="acc", bufs=4)
+            accs[i] = acc
+            nc.tensor.matmul_mx(
+                out=acc[:, : hi - lo],
+                lhsT=q_codes[:].bitcast(FP8X4),
+                lhsT_scale=q_scales[:],
+                rhs=codes[i][:].bitcast(FP8X4),
+                rhs_scale=scales[i][:],
+                start=True,
+                stop=True,
+            )
+
+        def finish(i):
+            lo, hi = CHUNKS[i]
+            nc.vector.tensor_tensor(result[i][:], accs[i][:, : hi - lo], bias_sb[:, lo:hi], ADD)
+            nc.sync.dma_start(out=out[0, :, lo:hi], in_=result[i][:])
+
+        last = len(CHUNKS)
+        for step in range(last + 2):
+            if step < last:
+                gather(3, *CHUNKS[step])
+                round_pair(1, step)
+            if step == 1:
+                quantize_q()
+            if 1 <= step <= last:
+                quantize(step - 1)
+                multiply(step - 1)
+            if step >= 2:
+                finish(step - 2)

@@ -20,7 +20,7 @@ PACK = 4
 FLOPS = 2 * NQ * D * N
 BYTES = 4 * (D * C + D * NQ + 2 * N + NQ * N) + 2 * 8 * N
 
-CHUNKS = ((0, 512), (512, 1024), (1024, 1536), (1536, 1792), (1792, 2048))
+CHUNKS = ((0, 256), (256, 768), (768, 1280), (1280, 1792), (1792, 2048))
 
 
 def tile_attend_pq_lin_bias_kernel(tc, qT, cb, norm, bias, offs, out):
@@ -29,8 +29,11 @@ def tile_attend_pq_lin_bias_kernel(tc, qT, cb, norm, bias, offs, out):
         tc.tile_pool(name="held", bufs=1) as held,
         tc.psum_pool(name="psum", bufs=1) as psum,
     ):
-        norm16 = held.tile([P, 2, 8], F32, name="norm16")
-        nc.sync.dma_start(out=norm16[:], in_=norm[0:1, :].rearrange("o (b p m) -> p (o b) m", b=2, m=8))
+        norm8 = []
+        for b in range(2):
+            part = held.tile([P, 8], F32, name=f"norm8_{b}")
+            nc.sync.dma_start(out=part[:], in_=norm[0:1, 1024 * b : 1024 * (b + 1)].rearrange("o (p m) -> (o p) m", m=8))
+            norm8.append(part)
         offsets = held.tile([P, N // 16], U16, name="offsets")
         nc.sync.dma_start(offsets[:], offs)
 
@@ -47,18 +50,25 @@ def tile_attend_pq_lin_bias_kernel(tc, qT, cb, norm, bias, offs, out):
 
         ident = held.tile([P, P], F32, name="ident")
         make_identity(nc, ident[:])
-        norm_rep = held.tile([P, N], F32, name="norm_rep")
-        norm_view = norm_rep[:].rearrange("p (b j h m) -> p b h j m", b=2, h=2, m=4)
+        banks = []
         for b in range(2):
             for h in range(2):
                 bank = psum.tile([P, 4, P], F32, name=f"norm_bank{b}{h}")
                 for m in range(4):
-                    col = norm16[:, b, 4 * h + m : 4 * h + m + 1]
+                    col = norm8[b][:, 4 * h + m : 4 * h + m + 1]
                     nc.tensor.transpose(bank[:, m, :], col.to_broadcast([P, P]), ident[:])
-                if b == 0:
-                    nc.vector.tensor_copy(out=norm_view[:, b, h], in_=bank[:].rearrange("p m j -> p j m"))
-                else:
-                    nc.scalar.copy(out=norm_view[:, b, h], in_=bank[:].rearrange("p m j -> p j m"))
+                banks.append(bank)
+
+        def spread(copy, b, dst):
+            view = dst.rearrange("p (j h m) -> p h j m", h=2, m=4)
+            for h in range(2):
+                copy(out=view[:, h], in_=banks[2 * b + h][:].rearrange("p m j -> p j m"))
+
+        norm_first = held.tile([P, 1024], F32, name="norm_first")
+        norm_rep = held.tile([P, N], F32, name="norm_rep")
+        spread(nc.vector.tensor_copy, 0, norm_first[:])
+        spread(nc.scalar.copy, 1, norm_rep[:, 1024:])
+        spread(nc.scalar.copy, 0, norm_rep[:, :1024])
 
         pairs = [held.tile([P, 2, N], F32, name=f"pair{h}") for h in range(2)]
         grouped, codes, scales = [], [], []
@@ -68,10 +78,11 @@ def tile_attend_pq_lin_bias_kernel(tc, qT, cb, norm, bias, offs, out):
             scales.append(held.tile([P, hi - lo], U8, name=f"scales{i}", align_bytes=64))
 
         def gather(t, lo, hi):
+            factors = norm_first if t == 0 and lo == 0 else norm_rep
             nc.vector.tensor_tensor(
                 pairs[t // 2][:, t % 2, lo:hi],
                 planes[t][:].indirect(offsets[:, lo // 16 : hi // 16]),
-                norm_rep[:, lo:hi],
+                factors[:, lo:hi],
                 MULT,
             )
 
@@ -131,15 +142,17 @@ def tile_attend_pq_lin_bias_kernel(tc, qT, cb, norm, bias, offs, out):
             nc.vector.tensor_tensor(result[i][:], accs[i][:, : hi - lo], bias_sb[:, lo:hi], ADD)
             nc.sync.dma_start(out=out[0, :, lo:hi], in_=result[i][:])
 
-        last = len(CHUNKS)
-        for step in range(last + 2):
-            if step < last:
-                gather(3, *CHUNKS[step])
-                round_pair(1, step)
-            if step == 1:
+        order = "G0 G1 q G2 Q0 G3 Q1 G4 B0 Q2 B1 Q3 B2 Q4 B3 B4"
+        for step in order.split(" "):
+            if step == "q":
                 quantize_q()
-            if 1 <= step <= last:
-                quantize(step - 1)
-                multiply(step - 1)
-            if step >= 2:
-                finish(step - 2)
+                continue
+            i = int(step[1:])
+            if step.startswith("G"):
+                gather(3, *CHUNKS[i])
+                round_pair(1, i)
+            elif step.startswith("Q"):
+                quantize(i)
+                multiply(i)
+            else:
+                finish(i)

import concourse.mybir as mybir
from concourse.masks import make_identity

F32 = mybir.dt.float32
BF16 = mybir.dt.bfloat16
U32 = mybir.dt.uint32
U16 = mybir.dt.uint16
U8 = mybir.dt.uint8
FP8X4 = mybir.dt.float8_e4m3fn_x4
MULT = mybir.AluOpType.mult
ADD = mybir.AluOpType.add

P = 128
D = 512
N = 2048
C = 4096
NQ = 128
PACK = 4

FLOPS = 2 * NQ * D * N
BYTES = 4 * (D * C + D * NQ + 2 * N + NQ * N) + 2 * 8 * N

CHUNKS = ((0, 256), (256, 768), (768, 1280), (1280, 1792), (1792, 2048))


def tile_attend_pq_lin_bias_kernel(tc, qT, cb, norm, bias, offs, out):
    nc = tc.nc
    with (
        tc.tile_pool(name="held", bufs=1) as held,
        tc.psum_pool(name="psum", bufs=1) as psum,
    ):
        norm8 = []
        for b in range(2):
            part = held.tile([P, 8], F32, name=f"norm8_{b}")
            nc.sync.dma_start(out=part[:], in_=norm[0:1, 1024 * b : 1024 * (b + 1)].rearrange("o (p m) -> (o p) m", m=8))
            norm8.append(part)
        offsets = held.tile([P, N // 16], U16, name="offsets")
        nc.sync.dma_start(offsets[:], offs)

        planes = []
        rows = cb.rearrange("(p t) c -> p t c", t=PACK)
        for t in range(PACK):
            plane = held.tile([P, C], F32, name=f"plane{t}")
            nc.sync.dma_start(out=plane[:], in_=rows[:, t, :])
            planes.append(plane)
        q_raw = held.tile([P, PACK, NQ], F32, name="q_raw")
        nc.sync.dma_start(out=q_raw[:], in_=qT[0].rearrange("(p t) q -> p t q", t=PACK))
        bias_sb = held.tile([P, N], F32, name="bias_sb")
        nc.sync.dma_start(out=bias_sb[:], in_=bias)

        ident = held.tile([P, P], F32, name="ident")
        make_identity(nc, ident[:])
        banks = []
        for b in range(2):
            for h in range(2):
                bank = psum.tile([P, 4, P], F32, name=f"norm_bank{b}{h}")
                for m in range(4):
                    col = norm8[b][:, 4 * h + m : 4 * h + m + 1]
                    nc.tensor.transpose(bank[:, m, :], col.to_broadcast([P, P]), ident[:])
                banks.append(bank)

        def spread(copy, b, dst):
            view = dst.rearrange("p (j h m) -> p h j m", h=2, m=4)
            for h in range(2):
                copy(out=view[:, h], in_=banks[2 * b + h][:].rearrange("p m j -> p j m"))

        norm_first = held.tile([P, 1024], F32, name="norm_first")
        norm_rep = held.tile([P, N], F32, name="norm_rep")
        spread(nc.vector.tensor_copy, 0, norm_first[:])
        spread(nc.scalar.copy, 1, norm_rep[:, 1024:])
        spread(nc.scalar.copy, 0, norm_rep[:, :1024])

        pairs = [held.tile([P, 2, N], F32, name=f"pair{h}") for h in range(2)]
        grouped, codes, scales = [], [], []
        for i, (lo, hi) in enumerate(CHUNKS):
            grouped.append(held.tile([P, hi - lo, PACK], BF16, name=f"grouped{i}", align_bytes=64))
            codes.append(held.tile([P, hi - lo], U32, name=f"codes{i}", align_bytes=64))
            scales.append(held.tile([P, hi - lo], U8, name=f"scales{i}", align_bytes=64))

        def gather(t, lo, hi):
            factors = norm_first if t == 0 and lo == 0 else norm_rep
            nc.vector.tensor_tensor(
                pairs[t // 2][:, t % 2, lo:hi],
                planes[t][:].indirect(offsets[:, lo // 16 : hi // 16]),
                factors[:, lo:hi],
                MULT,
            )

        def round_pair(h, i):
            lo, hi = CHUNKS[i]
            nc.scalar.copy(
                out=grouped[i][:, :, 2 * h : 2 * h + 2],
                in_=pairs[h][:, :, lo:hi].rearrange("p t c -> p c t"),
            )

        for t in range(3):
            for lo in range(0, N, 1024):
                gather(t, lo, lo + 1024)
            if t == 1:
                for i in range(len(CHUNKS)):
                    round_pair(0, i)

        q_grouped = held.tile([P, NQ, PACK], BF16, name="q_grouped", align_bytes=64)
        nc.scalar.copy(out=q_grouped[:], in_=q_raw[:].rearrange("p t q -> p q t"))
        q_codes = held.tile([P, NQ], U32, name="q_codes", align_bytes=64)
        q_scales = held.tile([P, NQ], U8, name="q_scales", align_bytes=64)

        def quantize_q():
            nc.vector.quantize_mx(
                out=q_codes[:].bitcast(FP8X4),
                scales=q_scales[:],
                in_=q_grouped[:].rearrange("p q t -> p (q t)"),
            )

        result = [held.tile([P, hi - lo], F32, name=f"result{i}") for i, (lo, hi) in enumerate(CHUNKS)]

        def quantize(i):
            nc.vector.quantize_mx(
                out=codes[i][:].bitcast(FP8X4),
                scales=scales[i][:],
                in_=grouped[i][:].rearrange("p c t -> p (c t)"),
            )

        accs = {}

        def multiply(i):
            lo, hi = CHUNKS[i]
            acc = psum.tile([P, 512], F32, name="acc", tag="acc", bufs=4)
            accs[i] = acc
            nc.tensor.matmul_mx(
                out=acc[:, : hi - lo],
                lhsT=q_codes[:].bitcast(FP8X4),
                lhsT_scale=q_scales[:],
                rhs=codes[i][:].bitcast(FP8X4),
                rhs_scale=scales[i][:],
                start=True,
                stop=True,
            )

        def finish(i):
            lo, hi = CHUNKS[i]
            nc.vector.tensor_tensor(result[i][:], accs[i][:, : hi - lo], bias_sb[:, lo:hi], ADD)
            nc.sync.dma_start(out=out[0, :, lo:hi], in_=result[i][:])

        order = "G0 G1 q G2 Q0 G3 Q1 G4 B0 Q2 B1 Q3 B2 Q4 B3 B4"
        for step in order.split(" "):
            if step == "q":
                quantize_q()
                continue
            i = int(step[1:])
            if step.startswith("G"):
                gather(3, *CHUNKS[i])
                round_pair(1, i)
            elif step.startswith("Q"):
                quantize(i)
                multiply(i)
            else:
                finish(i)
